import numpy as np
import ml_dtypes


def mxq(x, axis, fmt="e4m3"):
    dtype, down = {"e4m3": (ml_dtypes.float8_e4m3fn, 7), "e5m2": (ml_dtypes.float8_e5m2, 14)}[fmt]
    v = np.moveaxis(np.asarray(x, np.float32).astype(ml_dtypes.bfloat16).astype(np.float64), axis, -1)
    blocks = v.reshape(v.shape[:-1] + (-1, 32))
    amax = np.abs(blocks).max(-1, keepdims=True)
    byte = np.maximum(np.where(amax > 0, np.frexp(amax)[1] - 1 + 127, 0) - down, 1)
    scale = np.exp2(byte - 127.0)
    codes = (blocks / scale).astype(np.float32).astype(dtype).astype(np.float64)
    return np.moveaxis((codes * scale).reshape(v.shape), -1, axis)


WIDE = False


def mx_kscale(k):
    if not WIDE:
        return np.ones(k)
    levels = np.array([10, -10, 5, -5, 0])
    if k % 512:
        return np.exp2(np.random.permutation(np.resize(levels, k // 32))).repeat(32)
    a = np.empty((k // 512, 16))
    for p in range(k // 512):
        a[p, :8] = np.random.permutation(np.resize(levels, 8))
        for g in range(8):
            far = levels[np.abs(levels - a[p, g]) >= 10]
            a[p, g + 8] = far[np.random.randint(len(far))]
    return np.exp2(a.ravel()).repeat(32)


def f64(x):
    return np.asarray(x).astype(np.float64)


def striped(idx):
    return np.tile(idx.reshape(-1, 16).T, (8, 1)).astype(np.uint16)


def unstriped(offs):
    return offs[:16].T.reshape(-1).astype(np.int64)


E2M1 = np.array([0.0, 0.5, 1.0, 1.5, 2.0, 3.0, 4.0, 6.0, -0.0, -0.5, -1.0, -1.5, -2.0, -3.0, -4.0, -6.0])


def pack_weight(w, fmt):
    k, n = w.shape
    w = f64(np.asarray(w, np.float32).astype(ml_dtypes.bfloat16)).reshape(k // 32, 32, n)
    amax = np.abs(w).max(1)
    if fmt == "e4m3":
        byte = np.frexp(amax)[1] - 1 + 127 - 7
    else:
        mant, ex = np.frexp(amax / 6.0)
        byte = np.where(mant > 0.5, ex, ex - 1) + 127
    byte = np.clip(np.where(amax > 0, byte, 1), 1, 254)
    scaled = (w * np.exp2(127.0 - byte)[:, None, :]).reshape(k, n).astype(np.float32)
    by_word = np.ascontiguousarray(scaled.reshape(k // 512, 128, 4, n).transpose(0, 1, 3, 2))
    if fmt == "e4m3":
        words = by_word.astype(ml_dtypes.float8_e4m3fn).view(np.uint8)
    else:
        c = by_word.astype(ml_dtypes.float4_e2m1fn).view(np.uint8) & 0xF
        words = (c[..., 0::2] | (c[..., 1::2] << 4)).reshape(k // 512, 128, 2 * n)
    return np.ascontiguousarray(words), np.ascontiguousarray(byte.astype(np.uint8).reshape(k // 512, 16, n))


def unpack_weight(words, scales, fmt):
    g, _, n = scales.shape
    words = np.ascontiguousarray(words).reshape(g, 128, n, -1)
    if fmt == "e4m3":
        vals = words.view(ml_dtypes.float8_e4m3fn).astype(np.float64)
    else:
        nib = np.empty((g, 128, n, 4), np.uint8)
        nib[..., 0::2] = words & 0xF
        nib[..., 1::2] = words >> 4
        vals = E2M1[nib]
    vals = vals * np.repeat(np.exp2(scales.astype(np.float64) - 127.0), 8, axis=1)[..., None]
    return vals.transpose(0, 1, 3, 2).reshape(g * 512, n)


def pack_table4(v):
    words, scales = pack_weight(v, "e2m1")
    g, t = words.shape[0] // 2, v.shape[1]
    words = words.reshape(g, 2, 128, t, 2).transpose(0, 2, 3, 1, 4)
    return np.concatenate([words.reshape(g, -1), scales.reshape(g, -1)], axis=1)


def unpack_table4(tab):
    g, t = tab.shape[0], tab.shape[1] // 544
    words = tab[:, :512 * t].reshape(g, 128, t, 2, 2).transpose(0, 3, 1, 2, 4).reshape(2 * g, 128, 2 * t)
    return unpack_weight(words, tab[:, 512 * t:].reshape(2 * g, 16, t), "e2m1")


K, M, T, S = 3072, 256, 1024, 256


def setup_inputs():
    n = np.random.standard_normal
    s = mx_kscale(K)[:, None]
    return {
        "tab": pack_table4(n((K, T)) * s),
        "w": (n((K, M)) / np.sqrt(K) / s).astype(np.float32),
        "r": (n((256, 256))).astype(np.float32),
        "offs": striped(np.random.permutation(T)[:S]),
    }


def reference(tab, w, r, offs):
    tab_ = unpack_table4(tab)[:, unstriped(offs)]
    w_ = mxq(f64(w), 0, "e4m3")
    y = tab_.T @ w_
    return f64(r) + y

@@ -1,0 +1,132 @@
+from contextlib import ExitStack
+
+import concourse.mybir as mybir
+
+K, T, S, N = 3072, 1024, 256, 256
+FLOPS = 2 * K * S * N
+
+F32 = mybir.dt.float32
+BF16 = mybir.dt.bfloat16
+I32 = mybir.dt.int32
+U32 = mybir.dt.uint32
+U16 = mybir.dt.uint16
+U8 = mybir.dt.uint8
+FP8X4 = mybir.dt.float8_e4m3fn_x4
+FP4X4 = mybir.dt.float4_e2m1fn_x4
+
+P = 128
+K_PASS = 512
+PASSES = K // K_PASS
+PAIRS = PASSES // 2
+WORD_BYTES = 4 * P * T
+
+
+def tile_list_tab4_tm_res_kernel(tc, tab, w, r, offs, out):
+    nc = tc.nc
+    add = mybir.AluOpType.add
+    with ExitStack() as ctx:
+        held = ctx.enter_context(tc.tile_pool(name="held", bufs=1))
+        psum = ctx.enter_context(tc.psum_pool(name="psum", bufs=1))
+
+        offsets = held.tile([P, S // 16], U16, name="offsets")
+        nc.sync.dma_start(offsets[:], offs)
+
+        tab_scales = held.tile([P, PAIRS, T // 4], I32, name="tab_scales", align_bytes=64)
+        nc.vector.memset(tab_scales[:], 0)
+        scale_rows = tab[:, WORD_BYTES:].rearrange("m (h q t) -> h q m t", h=2, q=16)
+        for h in range(2):
+            queue = nc.scalar
+            for quad in range(4):
+                queue.dma_start(
+                    tab_scales[32 * quad + 4 * h : 32 * quad + 4 * h + 4, :, :],
+                    scale_rows[h, 4 * quad : 4 * quad + 4, :, :].bitcast(I32),
+                )
+
+        tab_words = [held.tile([P, T], I32, name=f"tab_words{m}", align_bytes=64) for m in range(PAIRS)]
+        w_raw = [held.tile([P, 4, N], F32, name=f"w_raw{c}", align_bytes=64) for c in range(PASSES)]
+
+        def load_words(m):
+            nc.sync.dma_start(tab_words[m][:], tab[m, 0:WORD_BYTES].rearrange("(p b) -> p b", p=P).bitcast(I32))
+
+        def load_w(c):
+            nc.sync.dma_start(w_raw[c][:], w[K_PASS * c : K_PASS * (c + 1), :].rearrange("(p j) n -> p j n", j=4))
+
+        for m in range(PAIRS):
+            load_w(m)
+            load_words(m)
+        for c in range(PAIRS, PASSES):
+            load_w(c)
+        r_sb = held.tile([P, 2, N], F32, name="r_sb")
+        nc.sync.dma_start(r_sb[:], r.rearrange("(a p) n -> p a n", p=P))
+
+        sums = [[psum.tile([P, 128], F32, name=f"sum{a}{b}") for b in range(2)] for a in range(2)]
+
+        picked_scales = [held.tile([P, PAIRS, S // 4], I32, name=f"picked_scales{h}", align_bytes=64) for h in range(2)]
+
+        def gather_scales(m):
+            nc.vector.tensor_copy(
+                picked_scales[0][:, m, :].bitcast(U8), tab_scales[:, m, :].bitcast(U8).indirect(offsets[:])
+            )
+
+        def gather_words(m):
+            g = held.tile([P, S], I32, name=f"picked_words{m}", align_bytes=64)
+            nc.vector.tensor_copy(g[:].bitcast(U32), tab_words[m][:].bitcast(U32).indirect(offsets[:]))
+            return g
+
+        def part_words(m, g):
+            parted = held.tile([P, 2, 2 * S], U8, name=f"parted{m}", align_bytes=64)
+            nc.vector.tensor_copy(parted[:].bitcast(U16), g[:].bitcast(U16).rearrange("p (s h) -> p h s", h=2))
+            return parted
+
+        def round_w(c, col, width, engine):
+            grouped = held.tile([P, width, 4], BF16, name=f"grouped{c}_{col}", align_bytes=64)
+            source = w_raw[c][:, :, col : col + width].rearrange("p j n -> p n j")
+            if engine == "scalar":
+                nc.scalar.copy(grouped[:], source)
+            else:
+                nc.vector.tensor_copy(grouped[:], source)
+            return grouped
+
+        def quantise(c, col, width, grouped):
+            codes = held.tile([P, width], U32, name=f"codes{c}_{col}", align_bytes=64)
+            scales = held.tile([P, width], U8, name=f"scales{c}_{col}", align_bytes=64)
+            nc.vector.quantize_mx(codes[:].bitcast(FP8X4), scales[:], grouped[:].rearrange("p n j -> p (n j)"))
+            return codes, scales
+
+        parted = {}
+        pieces = {c: [(0, 256, "scalar")] for c in range(PASSES)}
+        pieces[4] = [(0, 128, "vector"), (128, 128, "scalar")]
+        pieces[5] = [(0, 128, "vector"), (128, 128, "scalar")]
+
+        def multiply(c):
+            for col, width, engine in pieces[c]:
+                grouped = round_w(c, col, width, engine)
+                codes, scales = quantise(c, col, width, grouped)
+                for n0 in range(0, width, 128):
+                    for a in range(2):
+                        nc.tensor.matmul_mx(
+                            sums[a][(col + n0) // 128][:],
+                            lhsT=parted[c // 2][:, c % 2, 256 * a : 256 * (a + 1)].bitcast(FP4X4),
+                            lhsT_scale=picked_scales[c % 2][:, c // 2, 32 * a : 32 * (a + 1)].bitcast(U8),
+                            rhs=codes[:, n0 : n0 + 128].bitcast(FP8X4),
+                            rhs_scale=scales[:, n0 : n0 + 128],
+                            start=(c == 0),
+                            stop=(c == PASSES - 1),
+                        )
+
+        for m in range(PAIRS):
+            gather_scales(m)
+        nc.gpsimd.dma_start(picked_scales[1][0:112, :, :], picked_scales[0][4:116, :, :])
+        for m in range(PAIRS):
+            picked = gather_words(m)
+            parted[m] = part_words(m, picked)
+            multiply(2 * m)
+            multiply(2 * m + 1)
+
+        result = [held.tile([P, N], F32, name=f"result{a}") for a in range(2)]
+        for b in range(2):
+            for a in range(2):
+                cols = slice(128 * b, 128 * (b + 1))
+                nc.vector.tensor_tensor(result[a][:, cols], sums[a][b][:], r_sb[:, a, cols], add)
+        for a in range(2):
+            nc.sync.dma_start(out[128 * a : 128 * (a + 1), :], result[a][:])

@@ -33,28 +33,28 @@ def tile_list_tab4_tm_res_kernel(tc, tab, w, r, offs, out):
 
         tab_scales = held.tile([P, PAIRS, T // 4], I32, name="tab_scales", align_bytes=64)
         nc.vector.memset(tab_scales[:], 0)
-        scale_rows = tab[:, WORD_BYTES:].rearrange("m (h q t) -> h q m t", h=2, q=16)
-        for h in range(2):
-            queue = nc.scalar
-            for quad in range(4):
-                queue.dma_start(
-                    tab_scales[32 * quad + 4 * h : 32 * quad + 4 * h + 4, :, :],
-                    scale_rows[h, 4 * quad : 4 * quad + 4, :, :].bitcast(I32),
-                )
-
         tab_words = [held.tile([P, T], I32, name=f"tab_words{m}", align_bytes=64) for m in range(PAIRS)]
         w_raw = [held.tile([P, 4, N], F32, name=f"w_raw{c}", align_bytes=64) for c in range(PASSES)]
 
         def load_words(m):
-            nc.sync.dma_start(tab_words[m][:], tab[m, 0:WORD_BYTES].rearrange("(p b) -> p b", p=P).bitcast(I32))
+            nc.gpsimd.dma_start(tab_words[m][:], tab[m, 0:WORD_BYTES].rearrange("(p b) -> p b", p=P).bitcast(I32))
 
         def load_w(c):
             nc.sync.dma_start(w_raw[c][:], w[K_PASS * c : K_PASS * (c + 1), :].rearrange("(p j) n -> p j n", j=4))
 
+        order = (0, 2, 4, 1, 3, 5)
         for m in range(PAIRS):
-            load_w(m)
             load_words(m)
-        for c in range(PAIRS, PASSES):
+        load_w(0)
+        scale_rows = tab[:, WORD_BYTES:].rearrange("m (h q t) -> h q m t", h=2, q=16)
+        for h in range(2):
+            for quad in range(4):
+                nc.sync.dma_start(
+                    tab_scales[32 * quad + 4 * h : 32 * quad + 4 * h + 4, :, :],
+                    scale_rows[h, 4 * quad : 4 * quad + 4, :, :].bitcast(I32),
+                )
+
+        for c in order[1:]:
             load_w(c)
         r_sb = held.tile([P, 2, N], F32, name="r_sb")
         nc.sync.dma_start(r_sb[:], r.rearrange("(a p) n -> p a n", p=P))
@@ -95,7 +95,7 @@ def tile_list_tab4_tm_res_kernel(tc, tab, w, r, offs, out):
 
         parted = {}
         pieces = {c: [(0, 256, "scalar")] for c in range(PASSES)}
-        pieces[4] = [(0, 128, "vector"), (128, 128, "scalar")]
+        pieces[3] = [(0, 128, "vector"), (128, 128, "scalar")]
         pieces[5] = [(0, 128, "vector"), (128, 128, "scalar")]
 
         def multiply(c):
@@ -116,12 +116,13 @@ def tile_list_tab4_tm_res_kernel(tc, tab, w, r, offs, out):
 
         for m in range(PAIRS):
             gather_scales(m)
-        nc.gpsimd.dma_start(picked_scales[1][0:112, :, :], picked_scales[0][4:116, :, :])
+        nc.sync.dma_start(picked_scales[1][0:112, :, :], picked_scales[0][4:116, :, :])
         for m in range(PAIRS):
             picked = gather_words(m)
             parted[m] = part_words(m, picked)
-            multiply(2 * m)
-            multiply(2 * m + 1)
+            multiply(order[m])
+        for c in order[PAIRS:]:
+            multiply(c)
 
         result = [held.tile([P, N], F32, name=f"result{a}") for a in range(2)]
         for b in range(2):

@@ -32,31 +32,37 @@ def tile_list_tab4_tm_res_kernel(tc, tab, w, r, offs, out):
         nc.sync.dma_start(offsets[:], offs)
 
         tab_scales = held.tile([P, PAIRS, T // 4], I32, name="tab_scales", align_bytes=64)
+        tab_words = held.tile([P, PAIRS, T], I32, name="tab_words", align_bytes=64)
+        w_raw = held.tile([P, PASSES, 4, N], F32, name="w_raw", align_bytes=64)
+        r_sb = held.tile([P, 2, N], F32, name="r_sb")
         nc.vector.memset(tab_scales[:], 0)
-        tab_words = [held.tile([P, T], I32, name=f"tab_words{m}", align_bytes=64) for m in range(PAIRS)]
-        w_raw = [held.tile([P, 4, N], F32, name=f"w_raw{c}", align_bytes=64) for c in range(PASSES)]
+        nc.vector.memset(w_raw[:, 1:PASSES, 0, 0:1], 0.0)
+        nc.vector.memset(tab_words[:, 2, 0:1], 0)
+        nc.vector.memset(r_sb[:, 0, 0:1], 0.0)
+        scale_rows = tab[:, WORD_BYTES:].rearrange("m (h q t) -> h q m t", h=2, q=16)
 
-        def load_words(m):
-            nc.gpsimd.dma_start(tab_words[m][:], tab[m, 0:WORD_BYTES].rearrange("(p b) -> p b", p=P).bitcast(I32))
+        def load_words(m, queue):
+            queue.dma_start(tab_words[:, m, :], tab[m, 0:WORD_BYTES].rearrange("(p b) -> p b", p=P).bitcast(I32))
 
         def load_w(c):
-            nc.sync.dma_start(w_raw[c][:], w[K_PASS * c : K_PASS * (c + 1), :].rearrange("(p j) n -> p j n", j=4))
+            nc.sync.dma_start(w_raw[:, c, :, :], w[K_PASS * c : K_PASS * (c + 1), :].rearrange("(p j) n -> p j n", j=4))
 
-        order = (0, 2, 4, 1, 3, 5)
-        for m in range(PAIRS):
-            load_words(m)
         load_w(0)
-        scale_rows = tab[:, WORD_BYTES:].rearrange("m (h q t) -> h q m t", h=2, q=16)
+        load_words(0, nc.gpsimd)
+        load_words(1, nc.gpsimd)
         for h in range(2):
             for quad in range(4):
                 nc.sync.dma_start(
                     tab_scales[32 * quad + 4 * h : 32 * quad + 4 * h + 4, :, :],
                     scale_rows[h, 4 * quad : 4 * quad + 4, :, :].bitcast(I32),
                 )
-
-        for c in order[1:]:
+        load_w(2)
+        load_words(2, nc.sync)
+        for c in (4, 1, 3):
             load_w(c)
-        r_sb = held.tile([P, 2, N], F32, name="r_sb")
+        last_rows = w[K_PASS * (PASSES - 1) :, :].rearrange("(p j) n -> p j n", j=4)
+        for j in (0, 2):
+            nc.sync.dma_start(w_raw[:, PASSES - 1, j : j + 2, :], last_rows[:, j : j + 2, :])
         nc.sync.dma_start(r_sb[:], r.rearrange("(a p) n -> p a n", p=P))
 
         sums = [[psum.tile([P, 128], F32, name=f"sum{a}{b}") for b in range(2)] for a in range(2)]
@@ -70,7 +76,7 @@ def tile_list_tab4_tm_res_kernel(tc, tab, w, r, offs, out):
 
         def gather_words(m):
             g = held.tile([P, S], I32, name=f"picked_words{m}", align_bytes=64)
-            nc.vector.tensor_copy(g[:].bitcast(U32), tab_words[m][:].bitcast(U32).indirect(offsets[:]))
+            nc.vector.tensor_copy(g[:].bitcast(U32), tab_words[:, m, :].bitcast(U32).indirect(offsets[:]))
             return g
 
         def part_words(m, g):
@@ -78,14 +84,12 @@ def tile_list_tab4_tm_res_kernel(tc, tab, w, r, offs, out):
             nc.vector.tensor_copy(parted[:].bitcast(U16), g[:].bitcast(U16).rearrange("p (s h) -> p h s", h=2))
             return parted
 
-        def round_w(c, col, width, engine):
-            grouped = held.tile([P, width, 4], BF16, name=f"grouped{c}_{col}", align_bytes=64)
-            source = w_raw[c][:, :, col : col + width].rearrange("p j n -> p n j")
+        def round_w(c, cols, rows, grouped, engine):
+            source = w_raw[:, c, rows, cols].rearrange("p j n -> p n j")
             if engine == "scalar":
-                nc.scalar.copy(grouped[:], source)
+                nc.scalar.copy(grouped[:, :, rows], source)
             else:
-                nc.vector.tensor_copy(grouped[:], source)
-            return grouped
+                nc.vector.tensor_copy(grouped[:, :, rows], source)
 
         def quantise(c, col, width, grouped):
             codes = held.tile([P, width], U32, name=f"codes{c}_{col}", align_bytes=64)
@@ -94,35 +98,48 @@ def tile_list_tab4_tm_res_kernel(tc, tab, w, r, offs, out):
             return codes, scales
 
         parted = {}
-        pieces = {c: [(0, 256, "scalar")] for c in range(PASSES)}
-        pieces[3] = [(0, 128, "vector"), (128, 128, "scalar")]
-        pieces[5] = [(0, 128, "vector"), (128, 128, "scalar")]
+        every_row = slice(0, 4)
 
-        def multiply(c):
-            for col, width, engine in pieces[c]:
-                grouped = round_w(c, col, width, engine)
-                codes, scales = quantise(c, col, width, grouped)
-                for n0 in range(0, width, 128):
-                    for a in range(2):
-                        nc.tensor.matmul_mx(
-                            sums[a][(col + n0) // 128][:],
-                            lhsT=parted[c // 2][:, c % 2, 256 * a : 256 * (a + 1)].bitcast(FP4X4),
-                            lhsT_scale=picked_scales[c % 2][:, c // 2, 32 * a : 32 * (a + 1)].bitcast(U8),
-                            rhs=codes[:, n0 : n0 + 128].bitcast(FP8X4),
-                            rhs_scale=scales[:, n0 : n0 + 128],
-                            start=(c == 0),
-                            stop=(c == PASSES - 1),
-                        )
+        def multiply_piece(c, col, width, grouped):
+            codes, scales = quantise(c, col, width, grouped)
+            for n0 in range(0, width, 128):
+                for a in range(2):
+                    nc.tensor.matmul_mx(
+                        sums[a][(col + n0) // 128][:],
+                        lhsT=parted[c // 2][:, c % 2, 256 * a : 256 * (a + 1)].bitcast(FP4X4),
+                        lhsT_scale=picked_scales[c % 2][:, c // 2, 32 * a : 32 * (a + 1)].bitcast(U8),
+                        rhs=codes[:, n0 : n0 + 128].bitcast(FP8X4),
+                        rhs_scale=scales[:, n0 : n0 + 128],
+                        start=(c == 0),
+                        stop=(c == PASSES - 1),
+                    )
+
+        def multiply(c, shared):
+            grouped = held.tile([P, N, 4], BF16, name=f"grouped{c}", align_bytes=64)
+            if shared:
+                round_w(c, slice(0, 128), every_row, grouped[:, 0:128, :], "vector")
+                round_w(c, slice(128, N), every_row, grouped[:, 128:N, :], "scalar")
+            else:
+                round_w(c, slice(0, N), every_row, grouped[:], "scalar")
+            multiply_piece(c, 0, N, grouped)
+
+        def multiply_last():
+            halves = [held.tile([P, 128, 4], BF16, name=f"grouped_last{b}", align_bytes=64) for b in range(2)]
+            for rows in (slice(0, 2), slice(2, 4)):
+                round_w(PASSES - 1, slice(0, 128), rows, halves[0][:], "vector")
+                round_w(PASSES - 1, slice(128, N), rows, halves[1][:], "scalar")
+            for b in range(2):
+                multiply_piece(PASSES - 1, 128 * b, 128, halves[b])
 
         for m in range(PAIRS):
             gather_scales(m)
         nc.sync.dma_start(picked_scales[1][0:112, :, :], picked_scales[0][4:116, :, :])
         for m in range(PAIRS):
-            picked = gather_words(m)
-            parted[m] = part_words(m, picked)
-            multiply(order[m])
-        for c in order[PAIRS:]:
-            multiply(c)
+            parted[m] = part_words(m, gather_words(m))
+            multiply(2 * m, False)
+        multiply(1, True)
+        multiply(3, True)
+        multiply_last()
 
         result = [held.tile([P, N], F32, name=f"result{a}") for a in range(2)]
         for b in range(2):

@@ -31,35 +31,42 @@ def tile_list_tab4_tm_res_kernel(tc, tab, w, r, offs, out):
         offsets = held.tile([P, S // 16], U16, name="offsets")
         nc.sync.dma_start(offsets[:], offs)
 
-        tab_scales = held.tile([P, PAIRS, T // 4], I32, name="tab_scales", align_bytes=64)
+        tab_scales = [held.tile([P, PAIRS, T // 4], I32, name=f"tab_scales{h}", align_bytes=64) for h in range(2)]
         tab_words = held.tile([P, PAIRS, T], I32, name="tab_words", align_bytes=64)
         w_raw = held.tile([P, PASSES, 4, N], F32, name="w_raw", align_bytes=64)
         r_sb = held.tile([P, 2, N], F32, name="r_sb")
-        nc.vector.memset(tab_scales[:], 0)
+        for h in range(2):
+            nc.vector.memset(tab_scales[h][:], 0)
         nc.vector.memset(w_raw[:, 1:PASSES, 0, 0:1], 0.0)
-        nc.vector.memset(tab_words[:, 2, 0:1], 0)
+        nc.vector.memset(tab_words[:, :, 0:1], 0)
         nc.vector.memset(r_sb[:, 0, 0:1], 0.0)
         scale_rows = tab[:, WORD_BYTES:].rearrange("m (h q t) -> h q m t", h=2, q=16)
 
-        def load_words(m, queue):
-            queue.dma_start(tab_words[:, m, :], tab[m, 0:WORD_BYTES].rearrange("(p b) -> p b", p=P).bitcast(I32))
+        def load_words(m):
+            nc.sync.dma_start(tab_words[:, m, :], tab[m, 0:WORD_BYTES].rearrange("(p b) -> p b", p=P).bitcast(I32))
 
         def load_w(c):
             nc.sync.dma_start(w_raw[:, c, :, :], w[K_PASS * c : K_PASS * (c + 1), :].rearrange("(p j) n -> p j n", j=4))
 
         load_w(0)
-        load_words(0, nc.gpsimd)
-        load_words(1, nc.gpsimd)
-        for h in range(2):
-            for quad in range(4):
+
+        def load_scales(h, quads):
+            for quad in quads:
                 nc.sync.dma_start(
-                    tab_scales[32 * quad + 4 * h : 32 * quad + 4 * h + 4, :, :],
+                    tab_scales[h][32 * quad : 32 * quad + 4, :, :],
                     scale_rows[h, 4 * quad : 4 * quad + 4, :, :].bitcast(I32),
                 )
+
+        load_scales(0, range(4))
+        load_scales(1, range(1))
+        load_words(0)
         load_w(2)
-        load_words(2, nc.sync)
-        for c in (4, 1, 3):
-            load_w(c)
+        load_scales(1, range(1, 4))
+        load_words(1)
+        load_w(1)
+        load_w(4)
+        load_words(2)
+        load_w(3)
         last_rows = w[K_PASS * (PASSES - 1) :, :].rearrange("(p j) n -> p j n", j=4)
         for j in (0, 2):
             nc.sync.dma_start(w_raw[:, PASSES - 1, j : j + 2, :], last_rows[:, j : j + 2, :])
@@ -67,12 +74,11 @@ def tile_list_tab4_tm_res_kernel(tc, tab, w, r, offs, out):
 
         sums = [[psum.tile([P, 128], F32, name=f"sum{a}{b}") for b in range(2)] for a in range(2)]
 
-        picked_scales = [held.tile([P, PAIRS, S // 4], I32, name=f"picked_scales{h}", align_bytes=64) for h in range(2)]
+        picked_scales = [held.tile([P, S], U8, name=f"picked_scales{c}", align_bytes=64) for c in range(PASSES)]
 
-        def gather_scales(m):
-            nc.vector.tensor_copy(
-                picked_scales[0][:, m, :].bitcast(U8), tab_scales[:, m, :].bitcast(U8).indirect(offsets[:])
-            )
+        def gather_scales(c):
+            window = tab_scales[c % 2][:, c // 2, :].bitcast(U8)
+            nc.vector.tensor_copy(picked_scales[c][:], window.indirect(offsets[:]))
 
         def gather_words(m):
             g = held.tile([P, S], I32, name=f"picked_words{m}", align_bytes=64)
@@ -85,11 +91,12 @@ def tile_list_tab4_tm_res_kernel(tc, tab, w, r, offs, out):
             return parted
 
         def round_w(c, cols, rows, grouped, engine):
-            source = w_raw[:, c, rows, cols].rearrange("p j n -> p n j")
+            source = w_raw[:, c, rows, cols].rearrange("p j (g i) -> p g j i", i=4)
+            target = grouped[:, :, rows].rearrange("p (g i) j -> p g j i", i=4)
             if engine == "scalar":
-                nc.scalar.copy(grouped[:, :, rows], source)
+                nc.scalar.copy(target, source)
             else:
-                nc.vector.tensor_copy(grouped[:, :, rows], source)
+                nc.vector.tensor_copy(target, source)
 
         def quantise(c, col, width, grouped):
             codes = held.tile([P, width], U32, name=f"codes{c}_{col}", align_bytes=64)
@@ -107,7 +114,7 @@ def tile_list_tab4_tm_res_kernel(tc, tab, w, r, offs, out):
                     nc.tensor.matmul_mx(
                         sums[a][(col + n0) // 128][:],
                         lhsT=parted[c // 2][:, c % 2, 256 * a : 256 * (a + 1)].bitcast(FP4X4),
-                        lhsT_scale=picked_scales[c % 2][:, c // 2, 32 * a : 32 * (a + 1)].bitcast(U8),
+                        lhsT_scale=picked_scales[c][:, 128 * a : 128 * (a + 1)],
                         rhs=codes[:, n0 : n0 + 128].bitcast(FP8X4),
                         rhs_scale=scales[:, n0 : n0 + 128],
                         start=(c == 0),
@@ -131,14 +138,20 @@ def tile_list_tab4_tm_res_kernel(tc, tab, w, r, offs, out):
             for b in range(2):
                 multiply_piece(PASSES - 1, 128 * b, 128, halves[b])
 
-        for m in range(PAIRS):
-            gather_scales(m)
-        nc.sync.dma_start(picked_scales[1][0:112, :, :], picked_scales[0][4:116, :, :])
+        for c in (0, 2, 4):
+            gather_scales(c)
         for m in range(PAIRS):
             parted[m] = part_words(m, gather_words(m))
-            multiply(2 * m, False)
-        multiply(1, True)
-        multiply(3, True)
+            if m == 2:
+                gather_scales(3)
+                multiply(4, False)
+                gather_scales(5)
+                multiply(3, False)
+            else:
+                multiply(2 * m, False)
+            if m == 1:
+                gather_scales(1)
+                multiply(1, False)
         multiply_last()
 
         result = [held.tile([P, N], F32, name=f"result{a}") for a in range(2)]

from contextlib import ExitStack

import concourse.mybir as mybir

K, T, S, N = 3072, 1024, 256, 256
FLOPS = 2 * K * S * N

F32 = mybir.dt.float32
BF16 = mybir.dt.bfloat16
I32 = mybir.dt.int32
U32 = mybir.dt.uint32
U16 = mybir.dt.uint16
U8 = mybir.dt.uint8
FP8X4 = mybir.dt.float8_e4m3fn_x4
FP4X4 = mybir.dt.float4_e2m1fn_x4

P = 128
K_PASS = 512
PASSES = K // K_PASS
PAIRS = PASSES // 2
WORD_BYTES = 4 * P * T


def tile_list_tab4_tm_res_kernel(tc, tab, w, r, offs, out):
    nc = tc.nc
    add = mybir.AluOpType.add
    with ExitStack() as ctx:
        held = ctx.enter_context(tc.tile_pool(name="held", bufs=1))
        psum = ctx.enter_context(tc.psum_pool(name="psum", bufs=1))

        offsets = held.tile([P, S // 16], U16, name="offsets")
        nc.sync.dma_start(offsets[:], offs)

        tab_scales = [held.tile([P, PAIRS, T // 4], I32, name=f"tab_scales{h}", align_bytes=64) for h in range(2)]
        tab_words = held.tile([P, PAIRS, T], I32, name="tab_words", align_bytes=64)
        w_raw = held.tile([P, PASSES, 4, N], F32, name="w_raw", align_bytes=64)
        r_sb = held.tile([P, 2, N], F32, name="r_sb")
        for h in range(2):
            nc.vector.memset(tab_scales[h][:], 0)
        nc.vector.memset(w_raw[:, 1:PASSES, 0, 0:1], 0.0)
        nc.vector.memset(tab_words[:, :, 0:1], 0)
        nc.vector.memset(r_sb[:, 0, 0:1], 0.0)
        scale_rows = tab[:, WORD_BYTES:].rearrange("m (h q t) -> h q m t", h=2, q=16)

        def load_words(m):
            nc.sync.dma_start(tab_words[:, m, :], tab[m, 0:WORD_BYTES].rearrange("(p b) -> p b", p=P).bitcast(I32))

        def load_w(c):
            nc.sync.dma_start(w_raw[:, c, :, :], w[K_PASS * c : K_PASS * (c + 1), :].rearrange("(p j) n -> p j n", j=4))

        load_w(0)

        def load_scales(h, quads):
            for quad in quads:
                nc.sync.dma_start(
                    tab_scales[h][32 * quad : 32 * quad + 4, :, :],
                    scale_rows[h, 4 * quad : 4 * quad + 4, :, :].bitcast(I32),
                )

        load_scales(0, range(4))
        load_scales(1, range(1))
        load_words(0)
        load_w(2)
        load_scales(1, range(1, 4))
        load_words(1)
        load_w(1)
        load_w(4)
        load_words(2)
        load_w(3)
        last_rows = w[K_PASS * (PASSES - 1) :, :].rearrange("(p j) n -> p j n", j=4)
        for j in (0, 2):
            nc.sync.dma_start(w_raw[:, PASSES - 1, j : j + 2, :], last_rows[:, j : j + 2, :])
        nc.sync.dma_start(r_sb[:], r.rearrange("(a p) n -> p a n", p=P))

        sums = [[psum.tile([P, 128], F32, name=f"sum{a}{b}") for b in range(2)] for a in range(2)]

        picked_scales = [held.tile([P, S], U8, name=f"picked_scales{c}", align_bytes=64) for c in range(PASSES)]

        def gather_scales(c):
            window = tab_scales[c % 2][:, c // 2, :].bitcast(U8)
            nc.vector.tensor_copy(picked_scales[c][:], window.indirect(offsets[:]))

        def gather_words(m):
            g = held.tile([P, S], I32, name=f"picked_words{m}", align_bytes=64)
            nc.vector.tensor_copy(g[:].bitcast(U32), tab_words[:, m, :].bitcast(U32).indirect(offsets[:]))
            return g

        def part_words(m, g):
            parted = held.tile([P, 2, 2 * S], U8, name=f"parted{m}", align_bytes=64)
            nc.vector.tensor_copy(parted[:].bitcast(U16), g[:].bitcast(U16).rearrange("p (s h) -> p h s", h=2))
            return parted

        def round_w(c, cols, rows, grouped, engine):
            source = w_raw[:, c, rows, cols].rearrange("p j (g i) -> p g j i", i=4)
            target = grouped[:, :, rows].rearrange("p (g i) j -> p g j i", i=4)
            if engine == "scalar":
                nc.scalar.copy(target, source)
            else:
                nc.vector.tensor_copy(target, source)

        def quantise(c, col, width, grouped):
            codes = held.tile([P, width], U32, name=f"codes{c}_{col}", align_bytes=64)
            scales = held.tile([P, width], U8, name=f"scales{c}_{col}", align_bytes=64)
            nc.vector.quantize_mx(codes[:].bitcast(FP8X4), scales[:], grouped[:].rearrange("p n j -> p (n j)"))
            return codes, scales

        parted = {}
        every_row = slice(0, 4)

        def multiply_piece(c, col, width, grouped):
            codes, scales = quantise(c, col, width, grouped)
            for n0 in range(0, width, 128):
                for a in range(2):
                    nc.tensor.matmul_mx(
                        sums[a][(col + n0) // 128][:],
                        lhsT=parted[c // 2][:, c % 2, 256 * a : 256 * (a + 1)].bitcast(FP4X4),
                        lhsT_scale=picked_scales[c][:, 128 * a : 128 * (a + 1)],
                        rhs=codes[:, n0 : n0 + 128].bitcast(FP8X4),
                        rhs_scale=scales[:, n0 : n0 + 128],
                        start=(c == 0),
                        stop=(c == PASSES - 1),
                    )

        def multiply(c, shared):
            grouped = held.tile([P, N, 4], BF16, name=f"grouped{c}", align_bytes=64)
            if shared:
                round_w(c, slice(0, 128), every_row, grouped[:, 0:128, :], "vector")
                round_w(c, slice(128, N), every_row, grouped[:, 128:N, :], "scalar")
            else:
                round_w(c, slice(0, N), every_row, grouped[:], "scalar")
            multiply_piece(c, 0, N, grouped)

        def multiply_last():
            halves = [held.tile([P, 128, 4], BF16, name=f"grouped_last{b}", align_bytes=64) for b in range(2)]
            for rows in (slice(0, 2), slice(2, 4)):
                round_w(PASSES - 1, slice(0, 128), rows, halves[0][:], "vector")
                round_w(PASSES - 1, slice(128, N), rows, halves[1][:], "scalar")
            for b in range(2):
                multiply_piece(PASSES - 1, 128 * b, 128, halves[b])

        for c in (0, 2, 4):
            gather_scales(c)
        for m in range(PAIRS):
            parted[m] = part_words(m, gather_words(m))
            if m == 2:
                gather_scales(3)
                multiply(4, False)
                gather_scales(5)
                multiply(3, False)
            else:
                multiply(2 * m, False)
            if m == 1:
                gather_scales(1)
                multiply(1, False)
        multiply_last()

        result = [held.tile([P, N], F32, name=f"result{a}") for a in range(2)]
        for b in range(2):
            for a in range(2):
                cols = slice(128 * b, 128 * (b + 1))
                nc.vector.tensor_tensor(result[a][:, cols], sums[a][b][:], r_sb[:, a, cols], add)
        for a in range(2):
            nc.sync.dma_start(out[128 * a : 128 * (a + 1), :], result[a][:])
